import numpy as np
import ml_dtypes


def mxq(x, axis, fmt="e4m3"):
    dtype, down = {"e4m3": (ml_dtypes.float8_e4m3fn, 7), "e5m2": (ml_dtypes.float8_e5m2, 14)}[fmt]
    v = np.moveaxis(np.asarray(x, np.float32).astype(ml_dtypes.bfloat16).astype(np.float64), axis, -1)
    blocks = v.reshape(v.shape[:-1] + (-1, 32))
    amax = np.abs(blocks).max(-1, keepdims=True)
    byte = np.maximum(np.where(amax > 0, np.frexp(amax)[1] - 1 + 127, 0) - down, 1)
    scale = np.exp2(byte - 127.0)
    codes = (blocks / scale).astype(np.float32).astype(dtype).astype(np.float64)
    return np.moveaxis((codes * scale).reshape(v.shape), -1, axis)


WIDE = False


def mx_kscale(k):
    if not WIDE:
        return np.ones(k)
    levels = np.array([10, -10, 5, -5, 0])
    if k % 512:
        return np.exp2(np.random.permutation(np.resize(levels, k // 32))).repeat(32)
    a = np.empty((k // 512, 16))
    for p in range(k // 512):
        a[p, :8] = np.random.permutation(np.resize(levels, 8))
        for g in range(8):
            far = levels[np.abs(levels - a[p, g]) >= 10]
            a[p, g + 8] = far[np.random.randint(len(far))]
    return np.exp2(a.ravel()).repeat(32)


def f64(x):
    return np.asarray(x).astype(np.float64)


def striped(idx):
    return np.tile(idx.reshape(-1, 16).T, (8, 1)).astype(np.uint16)


def unstriped(offs):
    return offs[:16].T.reshape(-1).astype(np.int64)


def striped8(idx):
    return np.concatenate([x.reshape(-1, 16).T for x in idx]).astype(np.uint16)


def runs(offs, k):
    lists = np.stack([offs[16 * r : 16 * r + 16].T.reshape(-1) for r in range(8)]).astype(np.int64)
    return lists[np.arange(k) % 512 // 64]


def pack_weight(w):
    k, n = w.shape
    w = f64(np.asarray(w, np.float32).astype(ml_dtypes.bfloat16)).reshape(k // 32, 32, n)
    amax = np.abs(w).max(1)
    byte = np.clip(np.where(amax > 0, np.frexp(amax)[1] - 1 + 127 - 7, 1), 1, 254)
    scaled = (w * np.exp2(127.0 - byte)[:, None, :]).reshape(k, n).astype(np.float32)
    words = np.ascontiguousarray(scaled.reshape(k // 512, 128, 4, n).transpose(0, 1, 3, 2)).astype(ml_dtypes.float8_e4m3fn).view(np.uint8)
    return words, np.ascontiguousarray(byte.astype(np.uint8).reshape(k // 512, 16, n))


def unpack_weight(words, scales):
    g, p, n, _ = words.shape
    vals = np.ascontiguousarray(words).view(ml_dtypes.float8_e4m3fn).astype(np.float64) * np.repeat(np.exp2(scales.astype(np.float64) - 127.0), 8, axis=1)[..., None]
    return vals.transpose(0, 1, 3, 2).reshape(g * 512, n)


def sigmoid(v):
    return 1.0 / (1.0 + np.exp(-np.maximum(v, -700.0)))


K, T, S, V, H, W = 512, 2048, 512, 512, 512, 2048


def setup_inputs():
    n = np.random.standard_normal
    s = mx_kscale(K)[:, None]
    u = mx_kscale(S)
    packed_xT = pack_weight(n((K, T)) * s)
    return {
        "x_words": packed_xT[0],
        "x_scales": packed_xT[1],
        "w1": (n((K, H)) / np.sqrt(K) / s).astype(np.float32),
        "w2": (n((K, H)) / np.sqrt(K) / s).astype(np.float32),
        "w3": (n((K, H)) / np.sqrt(K) / s).astype(np.float32),
        "ga": (np.random.uniform(0.5, 1.5, (H, 1)) * u[:, None]).astype(np.float32),
        "gb": (np.random.uniform(0.5, 1.5, (H, 1)) / u[:, None]).astype(np.float32),
        "sl": np.random.uniform(1.0, 2.0, (S, 1)).astype(np.float32),
        "th": (0.5 * n((S, 1))).astype(np.float32),
        "sl2": np.random.uniform(1.0, 2.0, (S, 1)).astype(np.float32),
        "th2": (0.5 * n((S, 1))).astype(np.float32),
        "offs": striped(np.random.permutation(T)[:S]),
        "two": striped(np.random.permutation(T)[:S]),
        "n1": striped8(np.stack([np.random.permutation(S) for _ in range(8)])),
        "n2": striped8(np.stack([np.random.permutation(S) for _ in range(8)])),
        "n3": striped8(np.stack([np.random.permutation(S) for _ in range(8)])),
        "three": striped(np.random.permutation(T)[:V]),
        "n4": striped(np.random.randint(0, V, W)),
        "n5": striped(np.random.permutation(V)),
        "n6": striped(np.random.permutation(V)),
    }


def reference(x_words, x_scales, w1, w2, w3, ga, gb, sl, th, sl2, th2, offs, two, n1, n2, n3, three, n4, n5, n6):
    xq = unpack_weight(x_words, x_scales)[:, unstriped(offs)]
    y = mxq(f64(w1), 0, "e4m3").T @ xq
    x_two = unpack_weight(x_words, x_scales)[:, unstriped(two)]
    d = mxq(f64(w2), 0, "e4m3").T @ x_two
    z = f64(ga) * (np.maximum(np.minimum(y - (0.5 * (y[np.arange(H)[:, None], runs(n1, H)])), d[np.arange(H)[:, None], runs(n2, H)]), d[np.arange(H)[:, None], runs(n3, H)]))
    x_three = unpack_weight(x_words, x_scales)[:, unstriped(three)]
    b = mxq(f64(w3), 0, "e4m3").T @ x_three
    mb = b[:, unstriped(n4)]
    mx = mb.reshape(H, V, 4).max(axis=2)
    mn = mb.reshape(H, V, 4).min(axis=2)
    z2 = f64(gb) * (np.maximum(np.minimum(1.5 * b, mx), mn))
    s = 0.0625 * ((mxq(z, 0, "e4m3").T @ mxq(z2, 0, "e4m3")))
    sg = sigmoid(f64(sl) * (s[:, unstriped(n5)] - f64(th)))
    sg2 = sigmoid(f64(sl2) * (f64(th2) - s[:, unstriped(n6)]))
    return 2.0 * ((s * sg) * sg2)

@@ -1,0 +1,263 @@
+from contextlib import ExitStack
+
+import concourse.mybir as mybir
+
+F32 = mybir.dt.float32
+BF16 = mybir.dt.bfloat16
+I32 = mybir.dt.int32
+U32 = mybir.dt.uint32
+U16 = mybir.dt.uint16
+U8 = mybir.dt.uint8
+FP8X4 = mybir.dt.float8_e4m3fn_x4
+ALU = mybir.AluOpType
+ACT = mybir.ActivationFunctionType
+
+P = 128
+PACK = 4
+N = 512
+T = 2048
+HALF = N // 2
+MEMBERS = 4
+B_WINDOW = 1056
+FLOPS = 4 * 2 * 512 * 512 * 512
+
+
+def tile_picked_twkclampbgclipecr_none_p_kernel(tc, x_words, x_scales, w1, w2, w3, ga, gb, sl, th, sl2, th2, offs, two, n1, n2, n3, three, n4, n5, n6, out):
+    nc = tc.nc
+    with ExitStack() as ctx:
+        keep = ctx.enter_context(tc.tile_pool(name="keep", bufs=1))
+        ring = ctx.enter_context(tc.tile_pool(name="ring", bufs=2))
+        psum = ctx.enter_context(tc.psum_pool(name="psum", bufs=1))
+
+        def load_list(src, name):
+            tile = keep.tile(list(src.shape), U16, name=name)
+            nc.sync.dma_start(tile[:], src)
+            return tile
+
+        def load_half(w, name, h):
+            raw = keep.tile([P, PACK, HALF], F32, name=f"{name}_raw{h}")
+            nc.sync.dma_start(raw[:], w[:, h * HALF : (h + 1) * HALF].rearrange("(p j) c -> p j c", j=PACK))
+            return raw
+
+        xs = keep.tile([P, T], U8, name="xs")
+        nc.gpsimd.memset(xs[:].bitcast(I32), 0)
+        three_t = load_list(three, "three_t")
+        offs_t = load_list(offs, "offs_t")
+        two_t = load_list(two, "two_t")
+        w3_raw = [load_half(w3, "w3", 0)]
+        for q in range(4):
+            nc.sync.dma_start(xs[32 * q : 32 * q + 4, :].bitcast(I32), x_scales[0, 4 * q : 4 * q + 4, :].bitcast(I32))
+        w3_raw.append(load_half(w3, "w3", 1))
+        xw = keep.tile([P, T], U32, name="xw")
+        nc.sync.dma_start(xw[:].bitcast(I32), x_words[0].rearrange("p n t -> p (n t)").bitcast(I32))
+        n4_t = load_list(n4, "n4_t")
+        w1_raw = [load_half(w1, "w1", h) for h in range(2)]
+        w2_raw = [load_half(w2, "w2", h) for h in range(2)]
+        n1_t = load_list(n1, "n1_t")
+        n2_t = load_list(n2, "n2_t")
+        n3_t = load_list(n3, "n3_t")
+        n5_t = load_list(n5, "n5_t")
+        n6_t = load_list(n6, "n6_t")
+
+        ga_t = keep.tile([P, PACK], F32, name="ga_t")
+        gb_t = keep.tile([P, PACK], F32, name="gb_t")
+        nc.gpsimd.dma_start(ga_t[:], ga.rearrange("(p t) o -> p (t o)", t=PACK))
+        nc.gpsimd.dma_start(gb_t[:], gb.rearrange("(p t) o -> p (t o)", t=PACK))
+        rows = {}
+        with nc.allow_non_contiguous_dma(reason="one value a row of s"):
+            for name, src in (("sl", sl), ("th", th), ("sl2", sl2), ("th2", th2)):
+                rows[name] = keep.tile([P, 4], F32, name=f"{name}_t")
+                nc.sync.dma_start(rows[name][:], src.rearrange("(b p) o -> p (b o)", p=P))
+
+        half_sign = keep.tile([P, PACK], F32, name="half_sign")
+        sign = keep.tile([P, PACK], F32, name="sign")
+        ga_abs = keep.tile([P, PACK], F32, name="ga_abs")
+        gb_signed = keep.tile([P, PACK], F32, name="gb_signed")
+        nc.gpsimd.tensor_scalar(half_sign[:], ga_t[:], 0.0, 0.5, ALU.is_ge, ALU.subtract)
+        nc.gpsimd.tensor_scalar(sign[:], half_sign[:], 2.0, 0.0, ALU.mult, ALU.add)
+        nc.gpsimd.tensor_tensor(gb_signed[:], gb_t[:], sign[:], ALU.mult)
+        nc.gpsimd.tensor_tensor(ga_abs[:], ga_t[:], sign[:], ALU.mult)
+
+        b_win = []
+        for t in range(PACK):
+            win = keep.tile([P, B_WINDOW], F32, name=f"b_win{t}")
+            nc.gpsimd.memset(win[:, N:], 0.0)
+            b_win.append(win)
+
+        def pick_bytes(lst, name):
+            got = keep.tile([P, N], U8, name=f"{name}_bytes", align_bytes=64)
+            nc.vector.tensor_copy(got[:], xs[:].indirect(lst[:]))
+            return got
+
+        def pick_words(lst, name):
+            got = keep.tile([P, N], U32, name=f"{name}_words", align_bytes=64)
+            nc.vector.tensor_copy(got[:], xw[:].indirect(lst[:]))
+            return got
+
+        def deal(engine_copy, grouped, raw, h):
+            engine_copy(
+                grouped[:, :, h * 64 : (h + 1) * 64, :].rearrange("p t m j -> p m j t"),
+                raw[:].rearrange("p j (m t) -> p m j t", t=PACK),
+            )
+
+        def quantize(codes, scales, grouped):
+            nc.vector.quantize_mx(out=codes.bitcast(FP8X4), scales=scales, in_=grouped)
+
+        def mx_tiles(name):
+            grouped = keep.tile([P, PACK, P, PACK], BF16, name=f"{name}_bf", align_bytes=64)
+            codes = keep.tile([P, N], U32, name=f"{name}_codes", align_bytes=64)
+            scales = keep.tile([P, N], U8, name=f"{name}_scales", align_bytes=64)
+            return grouped, codes, scales
+
+        def product(bank, lhs_codes, lhs_scales, t, rhs_codes, rhs_scales):
+            acc = psum.tile([P, N], F32, name=f"bank{bank}")
+            cols = slice(t * P, (t + 1) * P)
+            nc.tensor.matmul_mx(out=acc[:], lhsT=lhs_codes[:, cols].bitcast(FP8X4), lhsT_scale=lhs_scales[:, cols],
+                                rhs=rhs_codes[:].bitcast(FP8X4), rhs_scale=rhs_scales[:], start=True, stop=True)
+            return acc
+
+        x3_bytes = pick_bytes(three_t, "x3")
+        x1_bytes = pick_bytes(offs_t, "x1")
+        x2_bytes = pick_bytes(two_t, "x2")
+        w3_bf, w3_codes, w3_scales = mx_tiles("w3")
+        for h in range(2):
+            deal(nc.scalar.copy, w3_bf, w3_raw[h], h)
+        quantize(w3_codes[:], w3_scales[:], w3_bf[:].rearrange("p t m j -> p (t m j)"))
+        x3_words = pick_words(three_t, "x3")
+        b_acc = [product(t, w3_codes, w3_scales, t, x3_words, x3_bytes) for t in range(PACK)]
+
+        members = []
+
+        def fetch_members(t):
+            nc.scalar.activation(b_win[t][:, :N], b_acc[t][:], ACT.Copy, scale=gb_signed[:, t : t + 1])
+            mb = keep.tile([P, N, MEMBERS], F32, name=f"mb{t}")
+            flat = mb[:].rearrange("p v m -> p (v m)")
+            for h in range(2):
+                nc.scalar.activation(flat[:, h * 1024 : (h + 1) * 1024], b_win[t][:].indirect(n4_t[:, h * 64 : (h + 1) * 64]), ACT.Copy)
+            members.append(mb)
+
+        for t in range(PACK):
+            fetch_members(t)
+        x1_words = pick_words(offs_t, "x1")
+        x2_words = pick_words(two_t, "x2")
+        w1_bf, w1_codes, w1_scales = mx_tiles("w1")
+        w2_bf, w2_codes, w2_scales = mx_tiles("w2")
+        for h in range(2):
+            deal(nc.vector.tensor_copy, w1_bf, w1_raw[h], h)
+        deal(nc.vector.tensor_copy, w2_bf, w2_raw[0], 0)
+        quantize(w1_codes[:], w1_scales[:], w1_bf[:].rearrange("p t m j -> p (t m j)"))
+        deal(nc.vector.tensor_copy, w2_bf, w2_raw[1], 1)
+        y_acc = [product(4 + t, w1_codes, w1_scales, t, x1_words, x1_bytes) for t in range(PACK)]
+        y_win, d_win = [], []
+        for t in range(PACK):
+            yw = keep.tile([P, N], F32, name=f"y_win{t}")
+            nc.vector.tensor_scalar(yw[:], y_acc[t][:], ga_abs[:, t : t + 1], None, ALU.mult)
+            y_win.append(yw)
+            if t == 0:
+                quantize(w2_codes[:], w2_scales[:], w2_bf[:].rearrange("p t m j -> p (t m j)"))
+        d_acc = [product(4 + t, w2_codes, w2_scales, t, x2_words, x2_bytes) for t in range(PACK)]
+        for t in range(PACK):
+            dw = keep.tile([P, N], F32, name=f"d_win{t}")
+            nc.vector.tensor_scalar(dw[:], d_acc[t][:], ga_abs[:, t : t + 1], None, ALU.mult)
+            d_win.append(dw)
+
+        below = keep.tile([P, PACK, N], F32, name="below")
+        least = keep.tile([P, PACK, N], F32, name="least")
+
+        def clamp(t):
+            mb = members[t]
+            hi = ring.tile([P, N, 2], F32, name="hi")
+            lo = ring.tile([P, N, 2], F32, name="lo")
+            most = ring.tile([P, N], F32, name="most")
+            for h in range(2):
+                v = slice(h * HALF, (h + 1) * HALF)
+                nc.vector.tensor_tensor(hi[:, v, :], mb[:, v, 0:2], mb[:, v, 2:4], ALU.max)
+                nc.vector.tensor_tensor(lo[:, v, :], mb[:, v, 0:2], mb[:, v, 2:4], ALU.min)
+            nc.vector.tensor_tensor(most[:], hi[:, :, 0], hi[:, :, 1], ALU.max)
+            nc.vector.tensor_tensor(least[:, t, :], lo[:, :, 0], lo[:, :, 1], ALU.min)
+            nc.vector.scalar_tensor_tensor(below[:, t, :], b_win[t][:, :N], 1.5, most[:], ALU.mult, ALU.min)
+
+        for t in range(PACK):
+            clamp(t)
+
+        def interleave(grouped, first, second):
+            nc.vector.tensor_tensor(
+                grouped.rearrange("p (c i) t -> p c t i", i=4),
+                first.rearrange("p t (c i) -> p c t i", i=4),
+                second.rearrange("p t (c i) -> p c t i", i=4),
+                ALU.max,
+            )
+
+        z2_bf = keep.tile([P, N, PACK], BF16, name="z2_bf", align_bytes=64)
+        z2_codes = keep.tile([P, N], U32, name="z2_codes", align_bytes=64)
+        z2_scales = keep.tile([P, N], U8, name="z2_scales", align_bytes=64)
+        interleave(z2_bf[:], below[:], least[:])
+
+        prod1 = keep.tile([P, 4], F32, name="prod1")
+        bias1 = keep.tile([P, 4], F32, name="bias1")
+        scale2 = keep.tile([P, 4], F32, name="scale2")
+        bias2 = keep.tile([P, 4], F32, name="bias2")
+        nc.gpsimd.tensor_tensor(prod1[:], rows["sl"][:], rows["th"][:], ALU.mult)
+        nc.gpsimd.tensor_scalar(bias1[:], prod1[:], -1.0, 0.0, ALU.mult, ALU.add)
+        nc.gpsimd.tensor_scalar(scale2[:], rows["sl2"][:], -1.0, 0.0, ALU.mult, ALU.add)
+        nc.gpsimd.tensor_tensor(bias2[:], rows["sl2"][:], rows["th2"][:], ALU.mult)
+
+        z_codes = keep.tile([P, N], U32, name="z_codes", align_bytes=64)
+        z_scales = keep.tile([P, N], U8, name="z_scales", align_bytes=64)
+        fetched = []
+
+        def fetch_keys(h):
+            lists = slice(h * 16, (h + 1) * 16)
+            y1 = ring.tile([P, PACK, HALF], F32, name="y1")
+            d2 = ring.tile([P, PACK, HALF], F32, name="d2")
+            d3 = ring.tile([P, PACK, HALF], F32, name="d3")
+            for t in range(PACK):
+                nc.scalar.activation(y1[:, t, :], y_win[t][:].indirect(n1_t[:, lists]), ACT.Copy)
+            for t in range(PACK):
+                nc.scalar.activation(d2[:, t, :], d_win[t][:].indirect(n2_t[:, lists]), ACT.Copy)
+            for t in range(PACK):
+                nc.scalar.activation(d3[:, t, :], d_win[t][:].indirect(n3_t[:, lists]), ACT.Copy)
+            fetched.append((y1, d2, d3))
+
+        def keys(h):
+            y1, d2, d3 = fetched[h]
+            j = slice(h * HALF, (h + 1) * HALF)
+            less = y1
+            for t in range(PACK):
+                nc.vector.scalar_tensor_tensor(less[:, t, :], y1[:, t, :], -0.5, y_win[t][:, j], ALU.mult, ALU.add)
+            nc.vector.tensor_tensor(less[:], less[:], d2[:], ALU.min)
+            z_bf = ring.tile([P, HALF, PACK], BF16, name="z_bf", align_bytes=64)
+            interleave(z_bf[:], less[:], d3[:])
+            quantize(z_codes[:, j], z_scales[:, j], z_bf[:].rearrange("p c t -> p (c t)"))
+
+        s_acc, s_win = {}, {}
+
+        def scores(b):
+            s_acc[b] = product(b, z_codes, z_scales, b, z2_codes, z2_scales)
+            s_win[b] = keep.tile([P, N], F32, name=f"s_win{b}")
+            nc.vector.tensor_scalar(s_win[b][:], s_acc[b][:], 0.0625, None, ALU.mult)
+
+        def finish(b):
+            sg = ring.tile([P, N], F32, name="sg")
+            sg2 = ring.tile([P, N], F32, name="sg2")
+            res = ring.tile([P, N], F32, name="res")
+            for h in range(2):
+                v = slice(h * HALF, (h + 1) * HALF)
+                lists = slice(h * 16, (h + 1) * 16)
+                nc.scalar.activation(sg[:, v], s_win[b][:].indirect(n5_t[:, lists]), ACT.Sigmoid, bias=bias1[:, b : b + 1], scale=rows["sl"][:, b : b + 1])
+                nc.scalar.activation(sg2[:, v], s_win[b][:].indirect(n6_t[:, lists]), ACT.Sigmoid, bias=bias2[:, b : b + 1], scale=scale2[:, b : b + 1])
+                nc.vector.tensor_tensor(sg[:, v], sg[:, v], sg2[:, v], ALU.mult)
+                nc.vector.scalar_tensor_tensor(res[:, v], s_acc[b][:, v], 0.125, sg[:, v], ALU.mult, ALU.mult)
+                nc.sync.dma_start(out[b * P : (b + 1) * P, v], res[:, v])
+
+        fetch_keys(0)
+        quantize(z2_codes[:], z2_scales[:], z2_bf[:].rearrange("p c t -> p (c t)"))
+        fetch_keys(1)
+        keys(0)
+        scores(0)
+        scores(1)
+        keys(1)
+        scores(2)
+        scores(3)
+        for b in range(4):
+            finish(b)

@@ -26,6 +26,8 @@ def tile_picked_twkclampbgclipecr_none_p_kernel(tc, x_words, x_scales, w1, w2, w
     nc = tc.nc
     with ExitStack() as ctx:
         keep = ctx.enter_context(tc.tile_pool(name="keep", bufs=1))
+        stage = ctx.enter_context(tc.tile_pool(name="stage", bufs=1))
+        raws = ctx.enter_context(tc.tile_pool(name="raws", bufs=1))
         ring = ctx.enter_context(tc.tile_pool(name="ring", bufs=2))
         psum = ctx.enter_context(tc.psum_pool(name="psum", bufs=1))
 
@@ -34,40 +36,39 @@ def tile_picked_twkclampbgclipecr_none_p_kernel(tc, x_words, x_scales, w1, w2, w
             nc.sync.dma_start(tile[:], src)
             return tile
 
-        def load_half(w, name, h):
-            raw = keep.tile([P, PACK, HALF], F32, name=f"{name}_raw{h}")
-            nc.sync.dma_start(raw[:], w[:, h * HALF : (h + 1) * HALF].rearrange("(p j) c -> p j c", j=PACK))
+        def load_weight(w, name, slot):
+            raw = raws.tile([P, PACK, N], F32, name=f"{name}_raw", offset=slot * 16 * N)
+            nc.sync.dma_start(raw[:], w.rearrange("(p j) c -> p j c", j=PACK))
             return raw
 
         xs = keep.tile([P, T], U8, name="xs")
         nc.gpsimd.memset(xs[:].bitcast(I32), 0)
         three_t = load_list(three, "three_t")
         offs_t = load_list(offs, "offs_t")
-        two_t = load_list(two, "two_t")
-        w3_raw = [load_half(w3, "w3", 0)]
         for q in range(4):
             nc.sync.dma_start(xs[32 * q : 32 * q + 4, :].bitcast(I32), x_scales[0, 4 * q : 4 * q + 4, :].bitcast(I32))
-        w3_raw.append(load_half(w3, "w3", 1))
+        w3_raw = load_weight(w3, "w3", 2)
         xw = keep.tile([P, T], U32, name="xw")
         nc.sync.dma_start(xw[:].bitcast(I32), x_words[0].rearrange("p n t -> p (n t)").bitcast(I32))
         n4_t = load_list(n4, "n4_t")
-        w1_raw = [load_half(w1, "w1", h) for h in range(2)]
-        w2_raw = [load_half(w2, "w2", h) for h in range(2)]
+        two_t = load_list(two, "two_t")
+        w1_raw = load_weight(w1, "w1", 1)
+        w2_raw = load_weight(w2, "w2", 0)
         n1_t = load_list(n1, "n1_t")
         n2_t = load_list(n2, "n2_t")
         n3_t = load_list(n3, "n3_t")
         n5_t = load_list(n5, "n5_t")
         n6_t = load_list(n6, "n6_t")
-
-        ga_t = keep.tile([P, PACK], F32, name="ga_t")
-        gb_t = keep.tile([P, PACK], F32, name="gb_t")
-        nc.gpsimd.dma_start(ga_t[:], ga.rearrange("(p t) o -> p (t o)", t=PACK))
-        nc.gpsimd.dma_start(gb_t[:], gb.rearrange("(p t) o -> p (t o)", t=PACK))
         rows = {}
         with nc.allow_non_contiguous_dma(reason="one value a row of s"):
             for name, src in (("sl", sl), ("th", th), ("sl2", sl2), ("th2", th2)):
                 rows[name] = keep.tile([P, 4], F32, name=f"{name}_t")
                 nc.sync.dma_start(rows[name][:], src.rearrange("(b p) o -> p (b o)", p=P))
+
+        ga_t = keep.tile([P, PACK], F32, name="ga_t")
+        gb_t = keep.tile([P, PACK], F32, name="gb_t")
+        nc.gpsimd.dma_start(ga_t[:], ga.rearrange("(p t) o -> p (t o)", t=PACK))
+        nc.gpsimd.dma_start(gb_t[:], gb.rearrange("(p t) o -> p (t o)", t=PACK))
 
         half_sign = keep.tile([P, PACK], F32, name="half_sign")
         sign = keep.tile([P, PACK], F32, name="sign")
@@ -78,33 +79,36 @@ def tile_picked_twkclampbgclipecr_none_p_kernel(tc, x_words, x_scales, w1, w2, w
         nc.gpsimd.tensor_tensor(gb_signed[:], gb_t[:], sign[:], ALU.mult)
         nc.gpsimd.tensor_tensor(ga_abs[:], ga_t[:], sign[:], ALU.mult)
 
-        b_win = []
+        b_win, s_win = [], []
         for t in range(PACK):
             win = keep.tile([P, B_WINDOW], F32, name=f"b_win{t}")
-            nc.gpsimd.memset(win[:, N:], 0.0)
+            nc.vector.memset(win[:, N:], 0.0)
             b_win.append(win)
+        for b in range(4):
+            s_win.append(keep.tile([P, 2 * N], F32, name=f"s_win{b}"))
 
-        def pick_bytes(lst, name):
-            got = keep.tile([P, N], U8, name=f"{name}_bytes", align_bytes=64)
+        def pick_bytes(lst, got):
             nc.vector.tensor_copy(got[:], xs[:].indirect(lst[:]))
             return got
 
-        def pick_words(lst, name):
-            got = keep.tile([P, N], U32, name=f"{name}_words", align_bytes=64)
+        def pick_words(lst, got):
             nc.vector.tensor_copy(got[:], xw[:].indirect(lst[:]))
             return got
 
-        def deal(engine_copy, grouped, raw, h):
+        def deal(engine_copy, grouped, raw, m=slice(0, P)):
             engine_copy(
-                grouped[:, :, h * 64 : (h + 1) * 64, :].rearrange("p t m j -> p m j t"),
-                raw[:].rearrange("p j (m t) -> p m j t", t=PACK),
+                grouped[:].rearrange("p t m j -> p m j t")[:, m],
+                raw[:].rearrange("p j (m t) -> p m j t", t=PACK)[:, m],
             )
+
+        def gpsimd_copy(dst, src):
+            nc.gpsimd.tensor_scalar(dst, src, 1.0, 0.0, ALU.mult, ALU.add)
 
         def quantize(codes, scales, grouped):
             nc.vector.quantize_mx(out=codes.bitcast(FP8X4), scales=scales, in_=grouped)
 
-        def mx_tiles(name):
-            grouped = keep.tile([P, PACK, P, PACK], BF16, name=f"{name}_bf", align_bytes=64)
+        def mx_tiles(name, slot):
+            grouped = stage.tile([P, PACK, P, PACK], BF16, name=f"{name}_bf", align_bytes=64, offset=(2 * N, 13 * N, 21 * N)[slot])
             codes = keep.tile([P, N], U32, name=f"{name}_codes", align_bytes=64)
             scales = keep.tile([P, N], U8, name=f"{name}_scales", align_bytes=64)
             return grouped, codes, scales
@@ -116,69 +120,63 @@ def tile_picked_twkclampbgclipecr_none_p_kernel(tc, x_words, x_scales, w1, w2, w
                                 rhs=rhs_codes[:].bitcast(FP8X4), rhs_scale=rhs_scales[:], start=True, stop=True)
             return acc
 
-        x3_bytes = pick_bytes(three_t, "x3")
-        x1_bytes = pick_bytes(offs_t, "x1")
-        x2_bytes = pick_bytes(two_t, "x2")
-        w3_bf, w3_codes, w3_scales = mx_tiles("w3")
-        for h in range(2):
-            deal(nc.scalar.copy, w3_bf, w3_raw[h], h)
+        def scaled_out(on_scalar, dst, acc, factor):
+            if on_scalar:
+                nc.scalar.activation(dst, acc, ACT.Copy, scale=factor)
+            else:
+                nc.vector.tensor_scalar(dst, acc, factor, None, ALU.mult)
+
+        x3_bytes = pick_bytes(three_t, keep.tile([P, N], U8, name="x3_bytes", align_bytes=64))
+        x1_bytes = pick_bytes(offs_t, keep.tile([P, N], U8, name="x1_bytes", align_bytes=64))
+        w3_bf, w3_codes, w3_scales = mx_tiles("w3", 0)
+        deal(nc.scalar.copy, w3_bf, w3_raw, slice(0, 64))
+        deal(nc.vector.tensor_copy, w3_bf, w3_raw, slice(64, P))
         quantize(w3_codes[:], w3_scales[:], w3_bf[:].rearrange("p t m j -> p (t m j)"))
-        x3_words = pick_words(three_t, "x3")
+        x3_words = pick_words(three_t, stage.tile([P, N], U32, name="x3_words", align_bytes=64, offset=4 * N))
         b_acc = [product(t, w3_codes, w3_scales, t, x3_words, x3_bytes) for t in range(PACK)]
 
         members = []
-
-        def fetch_members(t):
-            nc.scalar.activation(b_win[t][:, :N], b_acc[t][:], ACT.Copy, scale=gb_signed[:, t : t + 1])
+        for t in range(PACK):
+            scaled_out(True, b_win[t][:, :N], b_acc[t][:], gb_signed[:, t : t + 1])
             mb = keep.tile([P, N, MEMBERS], F32, name=f"mb{t}")
             flat = mb[:].rearrange("p v m -> p (v m)")
             for h in range(2):
                 nc.scalar.activation(flat[:, h * 1024 : (h + 1) * 1024], b_win[t][:].indirect(n4_t[:, h * 64 : (h + 1) * 64]), ACT.Copy)
             members.append(mb)
 
-        for t in range(PACK):
-            fetch_members(t)
-        x1_words = pick_words(offs_t, "x1")
-        x2_words = pick_words(two_t, "x2")
-        w1_bf, w1_codes, w1_scales = mx_tiles("w1")
-        w2_bf, w2_codes, w2_scales = mx_tiles("w2")
-        for h in range(2):
-            deal(nc.vector.tensor_copy, w1_bf, w1_raw[h], h)
-        deal(nc.vector.tensor_copy, w2_bf, w2_raw[0], 0)
+        x1_words = pick_words(offs_t, stage.tile([P, N], U32, name="x1_words", align_bytes=64, offset=0))
+        x2_words = pick_words(two_t, stage.tile([P, N], U32, name="x2_words", align_bytes=64, offset=9 * N))
+        x2_bytes = pick_bytes(two_t, stage.tile([P, N], U8, name="x2_bytes", align_bytes=64, offset=8 * N))
+        w1_bf, w1_codes, w1_scales = mx_tiles("w1", 1)
+        w2_bf, w2_codes, w2_scales = mx_tiles("w2", 2)
+        deal(nc.vector.tensor_copy, w1_bf, w1_raw)
+        deal(nc.vector.tensor_copy, w2_bf, w2_raw)
         quantize(w1_codes[:], w1_scales[:], w1_bf[:].rearrange("p t m j -> p (t m j)"))
-        deal(nc.vector.tensor_copy, w2_bf, w2_raw[1], 1)
+        quantize(w2_codes[:], w2_scales[:], w2_bf[:].rearrange("p t m j -> p (t m j)"))
         y_acc = [product(4 + t, w1_codes, w1_scales, t, x1_words, x1_bytes) for t in range(PACK)]
         y_win, d_win = [], []
         for t in range(PACK):
             yw = keep.tile([P, N], F32, name=f"y_win{t}")
-            nc.vector.tensor_scalar(yw[:], y_acc[t][:], ga_abs[:, t : t + 1], None, ALU.mult)
+            scaled_out(t < 0, yw[:], y_acc[t][:], ga_abs[:, t : t + 1])
             y_win.append(yw)
-            if t == 0:
-                quantize(w2_codes[:], w2_scales[:], w2_bf[:].rearrange("p t m j -> p (t m j)"))
         d_acc = [product(4 + t, w2_codes, w2_scales, t, x2_words, x2_bytes) for t in range(PACK)]
         for t in range(PACK):
             dw = keep.tile([P, N], F32, name=f"d_win{t}")
-            nc.vector.tensor_scalar(dw[:], d_acc[t][:], ga_abs[:, t : t + 1], None, ALU.mult)
+            scaled_out(t < 0, dw[:], d_acc[t][:], ga_abs[:, t : t + 1])
             d_win.append(dw)
 
         below = keep.tile([P, PACK, N], F32, name="below")
         least = keep.tile([P, PACK, N], F32, name="least")
-
-        def clamp(t):
-            mb = members[t]
-            hi = ring.tile([P, N, 2], F32, name="hi")
-            lo = ring.tile([P, N, 2], F32, name="lo")
-            most = ring.tile([P, N], F32, name="most")
-            for h in range(2):
-                v = slice(h * HALF, (h + 1) * HALF)
-                nc.vector.tensor_tensor(hi[:, v, :], mb[:, v, 0:2], mb[:, v, 2:4], ALU.max)
-                nc.vector.tensor_tensor(lo[:, v, :], mb[:, v, 0:2], mb[:, v, 2:4], ALU.min)
-            nc.vector.tensor_tensor(most[:], hi[:, :, 0], hi[:, :, 1], ALU.max)
-            nc.vector.tensor_tensor(least[:, t, :], lo[:, :, 0], lo[:, :, 1], ALU.min)
-            nc.vector.scalar_tensor_tensor(below[:, t, :], b_win[t][:, :N], 1.5, most[:], ALU.mult, ALU.min)
-
         for t in range(PACK):
-            clamp(t)
+            mb = members[t][:].rearrange("p (u e) m -> p u e m", e=2)
+            hi = raws.tile([P, N // 2, 2, 2], F32, name=f"hi{t}", offset=(t % 2) * 16 * N)
+            lo = raws.tile([P, N // 2, 2, 2], F32, name=f"lo{t}", offset=(t % 2) * 16 * N + 8 * N)
+            most = s_win[t][:, N:]
+            nc.vector.tensor_tensor(hi[:].rearrange("p u m e -> p u e m"), mb[:, :, :, 0:2], mb[:, :, :, 2:4], ALU.max)
+            nc.vector.tensor_tensor(lo[:].rearrange("p u m e -> p u e m"), mb[:, :, :, 0:2], mb[:, :, :, 2:4], ALU.min)
+            nc.vector.tensor_tensor(most.rearrange("p (u e) -> p u e", e=2), hi[:, :, 0, :], hi[:, :, 1, :], ALU.max)
+            nc.vector.tensor_tensor(least[:, t, :].rearrange("p (u e) -> p u e", e=2), lo[:, :, 0, :], lo[:, :, 1, :], ALU.min)
+            nc.vector.scalar_tensor_tensor(below[:, t, :], b_win[t][:, :N], 1.5, most, ALU.mult, ALU.min)
 
         def interleave(grouped, first, second):
             nc.vector.tensor_tensor(
@@ -204,60 +202,62 @@ def tile_picked_twkclampbgclipecr_none_p_kernel(tc, x_words, x_scales, w1, w2, w
 
         z_codes = keep.tile([P, N], U32, name="z_codes", align_bytes=64)
         z_scales = keep.tile([P, N], U8, name="z_scales", align_bytes=64)
-        fetched = []
+        less = keep.tile([P, PACK, N], F32, name="less")
+        d2 = keep.tile([P, PACK, N], F32, name="d2")
+        d3 = keep.tile([P, PACK, N], F32, name="d3")
+        z_bf = keep.tile([P, N, PACK], BF16, name="z_bf", align_bytes=64)
 
-        def fetch_keys(h):
-            lists = slice(h * 16, (h + 1) * 16)
-            y1 = ring.tile([P, PACK, HALF], F32, name="y1")
-            d2 = ring.tile([P, PACK, HALF], F32, name="d2")
-            d3 = ring.tile([P, PACK, HALF], F32, name="d3")
+        def fetch(dst, windows, lst, h, on_vector=0):
             for t in range(PACK):
-                nc.scalar.activation(y1[:, t, :], y_win[t][:].indirect(n1_t[:, lists]), ACT.Copy)
-            for t in range(PACK):
-                nc.scalar.activation(d2[:, t, :], d_win[t][:].indirect(n2_t[:, lists]), ACT.Copy)
-            for t in range(PACK):
-                nc.scalar.activation(d3[:, t, :], d_win[t][:].indirect(n3_t[:, lists]), ACT.Copy)
-            fetched.append((y1, d2, d3))
+                picked = windows[t][:].indirect(lst[:, h * 16 : (h + 1) * 16])
+                if t < on_vector:
+                    nc.vector.tensor_copy(dst[:, t, h * HALF : (h + 1) * HALF], picked)
+                else:
+                    nc.scalar.activation(dst[:, t, h * HALF : (h + 1) * HALF], picked, ACT.Copy)
 
-        def keys(h):
-            y1, d2, d3 = fetched[h]
-            j = slice(h * HALF, (h + 1) * HALF)
-            less = y1
-            for t in range(PACK):
-                nc.vector.scalar_tensor_tensor(less[:, t, :], y1[:, t, :], -0.5, y_win[t][:, j], ALU.mult, ALU.add)
-            nc.vector.tensor_tensor(less[:], less[:], d2[:], ALU.min)
-            z_bf = ring.tile([P, HALF, PACK], BF16, name="z_bf", align_bytes=64)
-            interleave(z_bf[:], less[:], d3[:])
-            quantize(z_codes[:, j], z_scales[:, j], z_bf[:].rearrange("p c t -> p (c t)"))
+        def keys(blocks):
+            cols = [slice(b * P, (b + 1) * P) for b in blocks]
+            for j in cols:
+                nc.vector.tensor_tensor(less[:, :, j], less[:, :, j], d2[:, :, j], ALU.min)
+            for j in cols:
+                interleave(z_bf[:, j, :], less[:, :, j], d3[:, :, j])
+            for j in cols:
+                quantize(z_codes[:, j], z_scales[:, j], z_bf[:, j, :].rearrange("p c t -> p (c t)"))
 
-        s_acc, s_win = {}, {}
+        s_acc = {}
 
         def scores(b):
             s_acc[b] = product(b, z_codes, z_scales, b, z2_codes, z2_scales)
-            s_win[b] = keep.tile([P, N], F32, name=f"s_win{b}")
-            nc.vector.tensor_scalar(s_win[b][:], s_acc[b][:], 0.0625, None, ALU.mult)
+            scaled_out(b < 0, s_win[b][:, :N], s_acc[b][:], 0.0625)
 
-        def finish(b):
-            sg = ring.tile([P, N], F32, name="sg")
-            sg2 = ring.tile([P, N], F32, name="sg2")
-            res = ring.tile([P, N], F32, name="res")
-            for h in range(2):
-                v = slice(h * HALF, (h + 1) * HALF)
-                lists = slice(h * 16, (h + 1) * 16)
+        def finish(b, pieces):
+            sg = keep.tile([P, N], F32, name=f"sg_{b}")
+            sg2 = keep.tile([P, N], F32, name=f"sg2_{b}")
+            res = keep.tile([P, N], F32, name=f"res_{b}")
+            width = N // pieces
+            for h in range(pieces):
+                v = slice(h * width, (h + 1) * width)
+                lists = slice(h * width // 16, (h + 1) * width // 16)
                 nc.scalar.activation(sg[:, v], s_win[b][:].indirect(n5_t[:, lists]), ACT.Sigmoid, bias=bias1[:, b : b + 1], scale=rows["sl"][:, b : b + 1])
                 nc.scalar.activation(sg2[:, v], s_win[b][:].indirect(n6_t[:, lists]), ACT.Sigmoid, bias=bias2[:, b : b + 1], scale=scale2[:, b : b + 1])
-                nc.vector.tensor_tensor(sg[:, v], sg[:, v], sg2[:, v], ALU.mult)
-                nc.vector.scalar_tensor_tensor(res[:, v], s_acc[b][:, v], 0.125, sg[:, v], ALU.mult, ALU.mult)
+                nc.vector.scalar_tensor_tensor(sg[:, v], s_acc[b][:, v], 0.125, sg[:, v], ALU.mult, ALU.mult)
+                nc.vector.tensor_tensor(res[:, v], sg[:, v], sg2[:, v], ALU.mult)
                 nc.sync.dma_start(out[b * P : (b + 1) * P, v], res[:, v])
 
-        fetch_keys(0)
-        quantize(z2_codes[:], z2_scales[:], z2_bf[:].rearrange("p c t -> p (c t)"))
-        fetch_keys(1)
-        keys(0)
+        for h in range(2):
+            fetch(less, y_win, n1_t, h)
+        for h in range(2):
+            fetch(d2, d_win, n2_t, h, 0 if h == 0 else 0)
+            fetch(d3, d_win, n3_t, h)
+        for t in range(PACK):
+            nc.vector.scalar_tensor_tensor(less[:, t, :], less[:, t, :], -0.5, y_win[t][:], ALU.mult, ALU.add)
+            if t == 0:
+                quantize(z2_codes[:], z2_scales[:], z2_bf[:].rearrange("p c t -> p (c t)"))
+        keys((0, 1))
         scores(0)
         scores(1)
-        keys(1)
+        keys((2, 3))
         scores(2)
         scores(3)
         for b in range(4):
-            finish(b)
+            finish(b, 2 if b == 3 else 1)

@@ -50,6 +50,10 @@ def tile_picked_twkclampbgclipecr_none_p_kernel(tc, x_words, x_scales, w1, w2, w
         w3_raw = load_weight(w3, "w3", 2)
         xw = keep.tile([P, T], U32, name="xw")
         nc.sync.dma_start(xw[:].bitcast(I32), x_words[0].rearrange("p n t -> p (n t)").bitcast(I32))
+        ga_t = keep.tile([P, PACK], F32, name="ga_t")
+        gb_t = keep.tile([P, PACK], F32, name="gb_t")
+        nc.sync.dma_start(ga_t[:], ga.rearrange("(p t) o -> p (t o)", t=PACK))
+        nc.sync.dma_start(gb_t[:], gb.rearrange("(p t) o -> p (t o)", t=PACK))
         n4_t = load_list(n4, "n4_t")
         two_t = load_list(two, "two_t")
         w1_raw = load_weight(w1, "w1", 1)
@@ -64,11 +68,6 @@ def tile_picked_twkclampbgclipecr_none_p_kernel(tc, x_words, x_scales, w1, w2, w
             for name, src in (("sl", sl), ("th", th), ("sl2", sl2), ("th2", th2)):
                 rows[name] = keep.tile([P, 4], F32, name=f"{name}_t")
                 nc.sync.dma_start(rows[name][:], src.rearrange("(b p) o -> p (b o)", p=P))
-
-        ga_t = keep.tile([P, PACK], F32, name="ga_t")
-        gb_t = keep.tile([P, PACK], F32, name="gb_t")
-        nc.gpsimd.dma_start(ga_t[:], ga.rearrange("(p t) o -> p (t o)", t=PACK))
-        nc.gpsimd.dma_start(gb_t[:], gb.rearrange("(p t) o -> p (t o)", t=PACK))
 
         half_sign = keep.tile([P, PACK], F32, name="half_sign")
         sign = keep.tile([P, PACK], F32, name="sign")
@@ -86,6 +85,8 @@ def tile_picked_twkclampbgclipecr_none_p_kernel(tc, x_words, x_scales, w1, w2, w
             b_win.append(win)
         for b in range(4):
             s_win.append(keep.tile([P, 2 * N], F32, name=f"s_win{b}"))
+        warm = keep.tile([P, 1], F32, name="warm")
+        nc.scalar.activation(warm[:], b_win[0][:, N : N + 1], ACT.Sigmoid)
 
         def pick_bytes(lst, got):
             nc.vector.tensor_copy(got[:], xs[:].indirect(lst[:]))
@@ -169,8 +170,8 @@ def tile_picked_twkclampbgclipecr_none_p_kernel(tc, x_words, x_scales, w1, w2, w
         least = keep.tile([P, PACK, N], F32, name="least")
         for t in range(PACK):
             mb = members[t][:].rearrange("p (u e) m -> p u e m", e=2)
-            hi = raws.tile([P, N // 2, 2, 2], F32, name=f"hi{t}", offset=(t % 2) * 16 * N)
-            lo = raws.tile([P, N // 2, 2, 2], F32, name=f"lo{t}", offset=(t % 2) * 16 * N + 8 * N)
+            hi = raws.tile([P, N // 2, 2, 2], F32, name=f"hi{t}", offset=0)
+            lo = raws.tile([P, N // 2, 2, 2], F32, name=f"lo{t}", offset=8 * N)
             most = s_win[t][:, N:]
             nc.vector.tensor_tensor(hi[:].rearrange("p u m e -> p u e m"), mb[:, :, :, 0:2], mb[:, :, :, 2:4], ALU.max)
             nc.vector.tensor_tensor(lo[:].rearrange("p u m e -> p u e m"), mb[:, :, :, 0:2], mb[:, :, :, 2:4], ALU.min)

@@ -69,15 +69,6 @@ def tile_picked_twkclampbgclipecr_none_p_kernel(tc, x_words, x_scales, w1, w2, w
                 rows[name] = keep.tile([P, 4], F32, name=f"{name}_t")
                 nc.sync.dma_start(rows[name][:], src.rearrange("(b p) o -> p (b o)", p=P))
 
-        half_sign = keep.tile([P, PACK], F32, name="half_sign")
-        sign = keep.tile([P, PACK], F32, name="sign")
-        ga_abs = keep.tile([P, PACK], F32, name="ga_abs")
-        gb_signed = keep.tile([P, PACK], F32, name="gb_signed")
-        nc.gpsimd.tensor_scalar(half_sign[:], ga_t[:], 0.0, 0.5, ALU.is_ge, ALU.subtract)
-        nc.gpsimd.tensor_scalar(sign[:], half_sign[:], 2.0, 0.0, ALU.mult, ALU.add)
-        nc.gpsimd.tensor_tensor(gb_signed[:], gb_t[:], sign[:], ALU.mult)
-        nc.gpsimd.tensor_tensor(ga_abs[:], ga_t[:], sign[:], ALU.mult)
-
         b_win, s_win = [], []
         for t in range(PACK):
             win = keep.tile([P, B_WINDOW], F32, name=f"b_win{t}")
@@ -98,8 +89,8 @@ def tile_picked_twkclampbgclipecr_none_p_kernel(tc, x_words, x_scales, w1, w2, w
 
         def deal(engine_copy, grouped, raw, m=slice(0, P)):
             engine_copy(
-                grouped[:].rearrange("p t m j -> p m j t")[:, m],
-                raw[:].rearrange("p j (m t) -> p m j t", t=PACK)[:, m],
+                grouped[:].rearrange("p t m j -> p m t j")[:, m],
+                raw[:].rearrange("p j (m t) -> p m t j", t=PACK)[:, m],
             )
 
         def gpsimd_copy(dst, src):
@@ -133,7 +124,13 @@ def tile_picked_twkclampbgclipecr_none_p_kernel(tc, x_words, x_scales, w1, w2, w
         deal(nc.scalar.copy, w3_bf, w3_raw, slice(0, 64))
         deal(nc.vector.tensor_copy, w3_bf, w3_raw, slice(64, P))
         quantize(w3_codes[:], w3_scales[:], w3_bf[:].rearrange("p t m j -> p (t m j)"))
+        half_sign = stage.tile([P, PACK], F32, name="half_sign", align_bytes=64, offset=8 * N)
+        nc.vector.tensor_scalar(half_sign[:], ga_t[:], 0.0, 0.5, ALU.is_ge, ALU.subtract)
         x3_words = pick_words(three_t, stage.tile([P, N], U32, name="x3_words", align_bytes=64, offset=4 * N))
+        gb_signed = keep.tile([P, PACK], F32, name="gb_signed")
+        ga_abs = keep.tile([P, PACK], F32, name="ga_abs")
+        nc.vector.scalar_tensor_tensor(gb_signed[:], gb_t[:], 2.0, half_sign[:], ALU.mult, ALU.mult)
+        nc.vector.scalar_tensor_tensor(ga_abs[:], ga_t[:], 2.0, half_sign[:], ALU.mult, ALU.mult)
         b_acc = [product(t, w3_codes, w3_scales, t, x3_words, x3_bytes) for t in range(PACK)]
 
         members = []
@@ -163,7 +160,7 @@ def tile_picked_twkclampbgclipecr_none_p_kernel(tc, x_words, x_scales, w1, w2, w
         d_acc = [product(4 + t, w2_codes, w2_scales, t, x2_words, x2_bytes) for t in range(PACK)]
         for t in range(PACK):
             dw = keep.tile([P, N], F32, name=f"d_win{t}")
-            scaled_out(t < 0, dw[:], d_acc[t][:], ga_abs[:, t : t + 1])
+            scaled_out(t < 1, dw[:], d_acc[t][:], ga_abs[:, t : t + 1])
             d_win.append(dw)
 
         below = keep.tile([P, PACK, N], F32, name="below")
@@ -192,14 +189,12 @@ def tile_picked_twkclampbgclipecr_none_p_kernel(tc, x_words, x_scales, w1, w2, w
         z2_scales = keep.tile([P, N], U8, name="z2_scales", align_bytes=64)
         interleave(z2_bf[:], below[:], least[:])
 
-        prod1 = keep.tile([P, 4], F32, name="prod1")
         bias1 = keep.tile([P, 4], F32, name="bias1")
         scale2 = keep.tile([P, 4], F32, name="scale2")
         bias2 = keep.tile([P, 4], F32, name="bias2")
-        nc.gpsimd.tensor_tensor(prod1[:], rows["sl"][:], rows["th"][:], ALU.mult)
-        nc.gpsimd.tensor_scalar(bias1[:], prod1[:], -1.0, 0.0, ALU.mult, ALU.add)
-        nc.gpsimd.tensor_scalar(scale2[:], rows["sl2"][:], -1.0, 0.0, ALU.mult, ALU.add)
-        nc.gpsimd.tensor_tensor(bias2[:], rows["sl2"][:], rows["th2"][:], ALU.mult)
+        nc.vector.scalar_tensor_tensor(bias1[:], rows["sl"][:], -1.0, rows["th"][:], ALU.mult, ALU.mult)
+        nc.vector.tensor_scalar(scale2[:], rows["sl2"][:], -1.0, None, ALU.mult)
+        nc.vector.tensor_tensor(bias2[:], rows["sl2"][:], rows["th2"][:], ALU.mult)
 
         z_codes = keep.tile([P, N], U32, name="z_codes", align_bytes=64)
         z_scales = keep.tile([P, N], U8, name="z_scales", align_bytes=64)

from contextlib import ExitStack

import concourse.mybir as mybir

F32 = mybir.dt.float32
BF16 = mybir.dt.bfloat16
I32 = mybir.dt.int32
U32 = mybir.dt.uint32
U16 = mybir.dt.uint16
U8 = mybir.dt.uint8
FP8X4 = mybir.dt.float8_e4m3fn_x4
ALU = mybir.AluOpType
ACT = mybir.ActivationFunctionType

P = 128
PACK = 4
N = 512
T = 2048
HALF = N // 2
MEMBERS = 4
B_WINDOW = 1056
FLOPS = 4 * 2 * 512 * 512 * 512


def tile_picked_twkclampbgclipecr_none_p_kernel(tc, x_words, x_scales, w1, w2, w3, ga, gb, sl, th, sl2, th2, offs, two, n1, n2, n3, three, n4, n5, n6, out):
    nc = tc.nc
    with ExitStack() as ctx:
        keep = ctx.enter_context(tc.tile_pool(name="keep", bufs=1))
        stage = ctx.enter_context(tc.tile_pool(name="stage", bufs=1))
        raws = ctx.enter_context(tc.tile_pool(name="raws", bufs=1))
        ring = ctx.enter_context(tc.tile_pool(name="ring", bufs=2))
        psum = ctx.enter_context(tc.psum_pool(name="psum", bufs=1))

        def load_list(src, name):
            tile = keep.tile(list(src.shape), U16, name=name)
            nc.sync.dma_start(tile[:], src)
            return tile

        def load_weight(w, name, slot):
            raw = raws.tile([P, PACK, N], F32, name=f"{name}_raw", offset=slot * 16 * N)
            nc.sync.dma_start(raw[:], w.rearrange("(p j) c -> p j c", j=PACK))
            return raw

        xs = keep.tile([P, T], U8, name="xs")
        nc.gpsimd.memset(xs[:].bitcast(I32), 0)
        three_t = load_list(three, "three_t")
        offs_t = load_list(offs, "offs_t")
        for q in range(4):
            nc.sync.dma_start(xs[32 * q : 32 * q + 4, :].bitcast(I32), x_scales[0, 4 * q : 4 * q + 4, :].bitcast(I32))
        w3_raw = load_weight(w3, "w3", 2)
        xw = keep.tile([P, T], U32, name="xw")
        nc.sync.dma_start(xw[:].bitcast(I32), x_words[0].rearrange("p n t -> p (n t)").bitcast(I32))
        ga_t = keep.tile([P, PACK], F32, name="ga_t")
        gb_t = keep.tile([P, PACK], F32, name="gb_t")
        nc.sync.dma_start(ga_t[:], ga.rearrange("(p t) o -> p (t o)", t=PACK))
        nc.sync.dma_start(gb_t[:], gb.rearrange("(p t) o -> p (t o)", t=PACK))
        n4_t = load_list(n4, "n4_t")
        two_t = load_list(two, "two_t")
        w1_raw = load_weight(w1, "w1", 1)
        w2_raw = load_weight(w2, "w2", 0)
        n1_t = load_list(n1, "n1_t")
        n2_t = load_list(n2, "n2_t")
        n3_t = load_list(n3, "n3_t")
        n5_t = load_list(n5, "n5_t")
        n6_t = load_list(n6, "n6_t")
        rows = {}
        with nc.allow_non_contiguous_dma(reason="one value a row of s"):
            for name, src in (("sl", sl), ("th", th), ("sl2", sl2), ("th2", th2)):
                rows[name] = keep.tile([P, 4], F32, name=f"{name}_t")
                nc.sync.dma_start(rows[name][:], src.rearrange("(b p) o -> p (b o)", p=P))

        b_win, s_win = [], []
        for t in range(PACK):
            win = keep.tile([P, B_WINDOW], F32, name=f"b_win{t}")
            nc.vector.memset(win[:, N:], 0.0)
            b_win.append(win)
        for b in range(4):
            s_win.append(keep.tile([P, 2 * N], F32, name=f"s_win{b}"))
        warm = keep.tile([P, 1], F32, name="warm")
        nc.scalar.activation(warm[:], b_win[0][:, N : N + 1], ACT.Sigmoid)

        def pick_bytes(lst, got):
            nc.vector.tensor_copy(got[:], xs[:].indirect(lst[:]))
            return got

        def pick_words(lst, got):
            nc.vector.tensor_copy(got[:], xw[:].indirect(lst[:]))
            return got

        def deal(engine_copy, grouped, raw, m=slice(0, P)):
            engine_copy(
                grouped[:].rearrange("p t m j -> p m t j")[:, m],
                raw[:].rearrange("p j (m t) -> p m t j", t=PACK)[:, m],
            )

        def gpsimd_copy(dst, src):
            nc.gpsimd.tensor_scalar(dst, src, 1.0, 0.0, ALU.mult, ALU.add)

        def quantize(codes, scales, grouped):
            nc.vector.quantize_mx(out=codes.bitcast(FP8X4), scales=scales, in_=grouped)

        def mx_tiles(name, slot):
            grouped = stage.tile([P, PACK, P, PACK], BF16, name=f"{name}_bf", align_bytes=64, offset=(2 * N, 13 * N, 21 * N)[slot])
            codes = keep.tile([P, N], U32, name=f"{name}_codes", align_bytes=64)
            scales = keep.tile([P, N], U8, name=f"{name}_scales", align_bytes=64)
            return grouped, codes, scales

        def product(bank, lhs_codes, lhs_scales, t, rhs_codes, rhs_scales):
            acc = psum.tile([P, N], F32, name=f"bank{bank}")
            cols = slice(t * P, (t + 1) * P)
            nc.tensor.matmul_mx(out=acc[:], lhsT=lhs_codes[:, cols].bitcast(FP8X4), lhsT_scale=lhs_scales[:, cols],
                                rhs=rhs_codes[:].bitcast(FP8X4), rhs_scale=rhs_scales[:], start=True, stop=True)
            return acc

        def scaled_out(on_scalar, dst, acc, factor):
            if on_scalar:
                nc.scalar.activation(dst, acc, ACT.Copy, scale=factor)
            else:
                nc.vector.tensor_scalar(dst, acc, factor, None, ALU.mult)

        x3_bytes = pick_bytes(three_t, keep.tile([P, N], U8, name="x3_bytes", align_bytes=64))
        x1_bytes = pick_bytes(offs_t, keep.tile([P, N], U8, name="x1_bytes", align_bytes=64))
        w3_bf, w3_codes, w3_scales = mx_tiles("w3", 0)
        deal(nc.scalar.copy, w3_bf, w3_raw, slice(0, 64))
        deal(nc.vector.tensor_copy, w3_bf, w3_raw, slice(64, P))
        quantize(w3_codes[:], w3_scales[:], w3_bf[:].rearrange("p t m j -> p (t m j)"))
        half_sign = stage.tile([P, PACK], F32, name="half_sign", align_bytes=64, offset=8 * N)
        nc.vector.tensor_scalar(half_sign[:], ga_t[:], 0.0, 0.5, ALU.is_ge, ALU.subtract)
        x3_words = pick_words(three_t, stage.tile([P, N], U32, name="x3_words", align_bytes=64, offset=4 * N))
        gb_signed = keep.tile([P, PACK], F32, name="gb_signed")
        ga_abs = keep.tile([P, PACK], F32, name="ga_abs")
        nc.vector.scalar_tensor_tensor(gb_signed[:], gb_t[:], 2.0, half_sign[:], ALU.mult, ALU.mult)
        nc.vector.scalar_tensor_tensor(ga_abs[:], ga_t[:], 2.0, half_sign[:], ALU.mult, ALU.mult)
        b_acc = [product(t, w3_codes, w3_scales, t, x3_words, x3_bytes) for t in range(PACK)]

        members = []
        for t in range(PACK):
            scaled_out(True, b_win[t][:, :N], b_acc[t][:], gb_signed[:, t : t + 1])
            mb = keep.tile([P, N, MEMBERS], F32, name=f"mb{t}")
            flat = mb[:].rearrange("p v m -> p (v m)")
            for h in range(2):
                nc.scalar.activation(flat[:, h * 1024 : (h + 1) * 1024], b_win[t][:].indirect(n4_t[:, h * 64 : (h + 1) * 64]), ACT.Copy)
            members.append(mb)

        x1_words = pick_words(offs_t, stage.tile([P, N], U32, name="x1_words", align_bytes=64, offset=0))
        x2_words = pick_words(two_t, stage.tile([P, N], U32, name="x2_words", align_bytes=64, offset=9 * N))
        x2_bytes = pick_bytes(two_t, stage.tile([P, N], U8, name="x2_bytes", align_bytes=64, offset=8 * N))
        w1_bf, w1_codes, w1_scales = mx_tiles("w1", 1)
        w2_bf, w2_codes, w2_scales = mx_tiles("w2", 2)
        deal(nc.vector.tensor_copy, w1_bf, w1_raw)
        deal(nc.vector.tensor_copy, w2_bf, w2_raw)
        quantize(w1_codes[:], w1_scales[:], w1_bf[:].rearrange("p t m j -> p (t m j)"))
        quantize(w2_codes[:], w2_scales[:], w2_bf[:].rearrange("p t m j -> p (t m j)"))
        y_acc = [product(4 + t, w1_codes, w1_scales, t, x1_words, x1_bytes) for t in range(PACK)]
        y_win, d_win = [], []
        for t in range(PACK):
            yw = keep.tile([P, N], F32, name=f"y_win{t}")
            scaled_out(t < 0, yw[:], y_acc[t][:], ga_abs[:, t : t + 1])
            y_win.append(yw)
        d_acc = [product(4 + t, w2_codes, w2_scales, t, x2_words, x2_bytes) for t in range(PACK)]
        for t in range(PACK):
            dw = keep.tile([P, N], F32, name=f"d_win{t}")
            scaled_out(t < 1, dw[:], d_acc[t][:], ga_abs[:, t : t + 1])
            d_win.append(dw)

        below = keep.tile([P, PACK, N], F32, name="below")
        least = keep.tile([P, PACK, N], F32, name="least")
        for t in range(PACK):
            mb = members[t][:].rearrange("p (u e) m -> p u e m", e=2)
            hi = raws.tile([P, N // 2, 2, 2], F32, name=f"hi{t}", offset=0)
            lo = raws.tile([P, N // 2, 2, 2], F32, name=f"lo{t}", offset=8 * N)
            most = s_win[t][:, N:]
            nc.vector.tensor_tensor(hi[:].rearrange("p u m e -> p u e m"), mb[:, :, :, 0:2], mb[:, :, :, 2:4], ALU.max)
            nc.vector.tensor_tensor(lo[:].rearrange("p u m e -> p u e m"), mb[:, :, :, 0:2], mb[:, :, :, 2:4], ALU.min)
            nc.vector.tensor_tensor(most.rearrange("p (u e) -> p u e", e=2), hi[:, :, 0, :], hi[:, :, 1, :], ALU.max)
            nc.vector.tensor_tensor(least[:, t, :].rearrange("p (u e) -> p u e", e=2), lo[:, :, 0, :], lo[:, :, 1, :], ALU.min)
            nc.vector.scalar_tensor_tensor(below[:, t, :], b_win[t][:, :N], 1.5, most, ALU.mult, ALU.min)

        def interleave(grouped, first, second):
            nc.vector.tensor_tensor(
                grouped.rearrange("p (c i) t -> p c t i", i=4),
                first.rearrange("p t (c i) -> p c t i", i=4),
                second.rearrange("p t (c i) -> p c t i", i=4),
                ALU.max,
            )

        z2_bf = keep.tile([P, N, PACK], BF16, name="z2_bf", align_bytes=64)
        z2_codes = keep.tile([P, N], U32, name="z2_codes", align_bytes=64)
        z2_scales = keep.tile([P, N], U8, name="z2_scales", align_bytes=64)
        interleave(z2_bf[:], below[:], least[:])

        bias1 = keep.tile([P, 4], F32, name="bias1")
        scale2 = keep.tile([P, 4], F32, name="scale2")
        bias2 = keep.tile([P, 4], F32, name="bias2")
        nc.vector.scalar_tensor_tensor(bias1[:], rows["sl"][:], -1.0, rows["th"][:], ALU.mult, ALU.mult)
        nc.vector.tensor_scalar(scale2[:], rows["sl2"][:], -1.0, None, ALU.mult)
        nc.vector.tensor_tensor(bias2[:], rows["sl2"][:], rows["th2"][:], ALU.mult)

        z_codes = keep.tile([P, N], U32, name="z_codes", align_bytes=64)
        z_scales = keep.tile([P, N], U8, name="z_scales", align_bytes=64)
        less = keep.tile([P, PACK, N], F32, name="less")
        d2 = keep.tile([P, PACK, N], F32, name="d2")
        d3 = keep.tile([P, PACK, N], F32, name="d3")
        z_bf = keep.tile([P, N, PACK], BF16, name="z_bf", align_bytes=64)

        def fetch(dst, windows, lst, h, on_vector=0):
            for t in range(PACK):
                picked = windows[t][:].indirect(lst[:, h * 16 : (h + 1) * 16])
                if t < on_vector:
                    nc.vector.tensor_copy(dst[:, t, h * HALF : (h + 1) * HALF], picked)
                else:
                    nc.scalar.activation(dst[:, t, h * HALF : (h + 1) * HALF], picked, ACT.Copy)

        def keys(blocks):
            cols = [slice(b * P, (b + 1) * P) for b in blocks]
            for j in cols:
                nc.vector.tensor_tensor(less[:, :, j], less[:, :, j], d2[:, :, j], ALU.min)
            for j in cols:
                interleave(z_bf[:, j, :], less[:, :, j], d3[:, :, j])
            for j in cols:
                quantize(z_codes[:, j], z_scales[:, j], z_bf[:, j, :].rearrange("p c t -> p (c t)"))

        s_acc = {}

        def scores(b):
            s_acc[b] = product(b, z_codes, z_scales, b, z2_codes, z2_scales)
            scaled_out(b < 0, s_win[b][:, :N], s_acc[b][:], 0.0625)

        def finish(b, pieces):
            sg = keep.tile([P, N], F32, name=f"sg_{b}")
            sg2 = keep.tile([P, N], F32, name=f"sg2_{b}")
            res = keep.tile([P, N], F32, name=f"res_{b}")
            width = N // pieces
            for h in range(pieces):
                v = slice(h * width, (h + 1) * width)
                lists = slice(h * width // 16, (h + 1) * width // 16)
                nc.scalar.activation(sg[:, v], s_win[b][:].indirect(n5_t[:, lists]), ACT.Sigmoid, bias=bias1[:, b : b + 1], scale=rows["sl"][:, b : b + 1])
                nc.scalar.activation(sg2[:, v], s_win[b][:].indirect(n6_t[:, lists]), ACT.Sigmoid, bias=bias2[:, b : b + 1], scale=scale2[:, b : b + 1])
                nc.vector.scalar_tensor_tensor(sg[:, v], s_acc[b][:, v], 0.125, sg[:, v], ALU.mult, ALU.mult)
                nc.vector.tensor_tensor(res[:, v], sg[:, v], sg2[:, v], ALU.mult)
                nc.sync.dma_start(out[b * P : (b + 1) * P, v], res[:, v])

        for h in range(2):
            fetch(less, y_win, n1_t, h)
        for h in range(2):
            fetch(d2, d_win, n2_t, h, 0 if h == 0 else 0)
            fetch(d3, d_win, n3_t, h)
        for t in range(PACK):
            nc.vector.scalar_tensor_tensor(less[:, t, :], less[:, t, :], -0.5, y_win[t][:], ALU.mult, ALU.add)
            if t == 0:
                quantize(z2_codes[:], z2_scales[:], z2_bf[:].rearrange("p c t -> p (c t)"))
        keys((0, 1))
        scores(0)
        scores(1)
        keys((2, 3))
        scores(2)
        scores(3)
        for b in range(4):
            finish(b, 2 if b == 3 else 1)
